import numpy as np
import ml_dtypes


def mxq(x, axis, fmt="e4m3"):
    dtype, down = {"e4m3": (ml_dtypes.float8_e4m3fn, 7), "e5m2": (ml_dtypes.float8_e5m2, 14)}[fmt]
    v = np.moveaxis(np.asarray(x, np.float32).astype(ml_dtypes.bfloat16).astype(np.float64), axis, -1)
    blocks = v.reshape(v.shape[:-1] + (-1, 32))
    amax = np.abs(blocks).max(-1, keepdims=True)
    byte = np.maximum(np.where(amax > 0, np.frexp(amax)[1] - 1 + 127, 0) - down, 1)
    scale = np.exp2(byte - 127.0)
    codes = (blocks / scale).astype(np.float32).astype(dtype).astype(np.float64)
    return np.moveaxis((codes * scale).reshape(v.shape), -1, axis)


WIDE = False


def mx_kscale(k):
    if not WIDE:
        return np.ones(k)
    levels = np.array([10, -10, 5, -5, 0])
    if k % 512:
        return np.exp2(np.random.permutation(np.resize(levels, k // 32))).repeat(32)
    a = np.empty((k // 512, 16))
    for p in range(k // 512):
        a[p, :8] = np.random.permutation(np.resize(levels, 8))
        for g in range(8):
            far = levels[np.abs(levels - a[p, g]) >= 10]
            a[p, g + 8] = far[np.random.randint(len(far))]
    return np.exp2(a.ravel()).repeat(32)


BF16 = ml_dtypes.bfloat16


def bf(x):
    return np.asarray(x, np.float32).astype(BF16)


def f64(x):
    return np.asarray(x).astype(np.float64)

def planes(Y):
    n, m = Y.shape
    b = f64(bf(Y)).reshape(n // 32, 32, m)
    amax = np.abs(b).max(1)
    byte = np.clip(np.where(amax > 0, np.frexp(amax)[1] - 1 + 127 - 7, 1), 1, 254)
    codes = (b * np.exp2(127.0 - byte)[:, None, :]).reshape(n, m).astype(np.float32).astype(ml_dtypes.float8_e4m3fn).view(np.uint8)
    words = codes.reshape(n // 512, 128, 4, m).transpose(0, 1, 3, 2)
    return np.ascontiguousarray(words), np.ascontiguousarray(byte.astype(np.uint8).reshape(n // 512, 16, m))


M, N, K_CAM, K_LID = 2048, 1024, 1024, 512
SPREAD = 0.8
CAM_LEVEL = 0.5
LID_LEVEL = 0.8
PRED_LEVEL = 0.5


def setup_inputs():
    s_cam = mx_kscale(K_CAM)
    s_lid = mx_kscale(K_LID)
    z_cam = np.random.randn(M, K_CAM)
    z_lid = np.random.randn(M, K_LID)
    h_cam = np.random.randn(K_CAM, N) / np.sqrt(K_CAM)
    h_lid = np.random.randn(K_LID, N) / np.sqrt(K_LID)
    lam_pred = PRED_LEVEL * np.exp(SPREAD * np.random.randn(M))
    return {
        "z_cam": bf(z_cam * s_cam[None, :]),
        "h_cam": bf(h_cam / s_cam[:, None]),
        "z_lid": bf(z_lid * s_lid[None, :]),
        "h_lid": bf(h_lid / s_lid[:, None]),
        "lam_cam": bf(CAM_LEVEL * np.exp(SPREAD * np.random.randn(M))),
        "lam_lid": bf(LID_LEVEL * np.exp(SPREAD * np.random.randn(M))),
        "eta_pred": bf(lam_pred[:, None] * np.random.randn(M, N)),
    }


def reference(z_cam, h_cam, z_lid, h_lid, lam_cam, lam_lid, eta_pred):
    x_cam = mxq(f64(z_cam), 1, "e4m3") @ mxq(f64(h_cam), 0, "e4m3")
    x_lid = mxq(f64(z_lid), 1, "e4m3") @ mxq(f64(h_lid), 0, "e4m3")
    y = f64(lam_cam)[:, None] * x_cam + f64(lam_lid)[:, None] * x_lid + f64(eta_pred)
    Y = y.reshape(M, N)
    words, scales = planes(Y)
    return y, words, scales

@@ -1,0 +1,264 @@
+from contextlib import ExitStack
+
+import concourse.mybir as mybir
+from concourse.masks import make_identity
+
+M, N, K_CAM, K_LID = 2048, 1024, 1024, 512
+FLOPS = 2 * M * N * (K_CAM + K_LID)
+
+F32 = mybir.dt.float32
+BF16 = mybir.dt.bfloat16
+U32 = mybir.dt.uint32
+I32 = mybir.dt.int32
+U8 = mybir.dt.uint8
+FP8X4 = mybir.dt.float8_e4m3fn_x4
+ALU = mybir.AluOpType
+ACT = mybir.ActivationFunctionType
+
+P = 128
+PACK = 4
+GROUP = P * PACK
+GROUPS = M // GROUP
+HALF = 512
+HALVES = N // HALF
+CAM_PASSES = K_CAM // GROUP
+TILES = GROUPS * HALVES * PACK
+
+UNITS = [(0, 0, 512), (1, 0, 512), (0, 512, 512), (1, 512, 512), (2, 0, 512), (2, 512, 512), (3, 0, 512), (3, 512, 256), (3, 768, 256)]
+LEAD = 4
+TURN_AHEAD = 8
+QUANT_AHEAD = 2
+H_AHEAD = 10
+PLANE_LAG = 8
+ASSIST = ()
+ASSIST_FROM = 1
+H_ENG = "VSVSSS"
+SPLIT = 44
+ACC = 6
+GADD = 512
+GPART = 32
+LOADS = "hl00 zl0 hc00 eta00 hc10 zc00 zc01 zl1 eta10 zc10 zc11 hl01 eta01 hc01 hc11 eta11 zl2 eta20 zc20 zc21 eta21 zl3 eta30 zc30 zc31 eta31"
+PLAN = "Vhl00 Tzl0 M Qhl00 Vhc00 Qzl0 Qhc00 L0 L1 L2 L3 Ihc10:0:304:S Tzc00 Ihc10:304:512:V Tzc01 Qzc00 Qhc10 C0 Qzc01 Tzl1 C1 C2 Qzl1 C3 Tzc10 L4 L5 Tzc11 Qzc10 L6 Shl01 L7 C4 Qzc11 C5 Shc01 C6 Qhl01 C7 Shc11 L8 L9 Qhc01 L10 Tzl2 L11 L12 Qhc11 L13 Tzc20 R0:0:256:S L14 C8 R0:256:512:S Qzl2 L15 C9 R1:0:256:S C10 Y0 Tzc21 R1:256:512:S C11 Qzc20 C12 R2:0:256:S C13 Y1 R2:256:512:S C14 Qzc21 L16 C15 Y2 Tzl3 R3:0:256:S R3:256:512:S L17 C16 L18 C17 L19 C18 Y3 Tzc30 Qzl3 L20 C19 L21 C20 Tzc31 R4:0:256:S R4:256:512:S L22 C21 Qzc30 L23 C22 Qzc31 L24 C23 R5:0:256:S R5:256:512:S Y4 L25 C24 L26 C25 L27 C26 Y5 L28 C27 R6:0:256:S R6:256:512:S L29 C28 L30 C29 L31 C30 L32 C31 L33 R7:0:256:S L34 c32 L35 c33 Y6 Z0:512:ssss c34 c35 R8:0:84:S Y7 R8:84:256:V Y8 Z512:1024:aass"
+
+
+def parse(word):
+    n = 3 if word.startswith("eta") else 2
+    return (word[:n],) + tuple(int(c) for c in word[n:])
+
+
+def tile_camera_lidar_information_fusion_g2_kernel(
+    tc, z_cam, h_cam, z_lid, h_lid, lam_cam, lam_lid, eta_pred, out_0, out_1, out_2
+):
+    nc = tc.nc
+    with ExitStack() as ctx:
+        keep = ctx.enter_context(tc.tile_pool(name="keep", bufs=1))
+        ring = ctx.enter_context(tc.tile_pool(name="ring", bufs=2))
+        psum = ctx.enter_context(tc.psum_pool(name="psum", bufs=1))
+        ctx.enter_context(tc.manual_schedule())
+
+        ident = keep.tile([P, P], F32, name="ident")
+        make_identity(nc, ident[:])
+
+        raw = {}
+
+        def load_z(key):
+            g = key[1]
+            if key[0] == "zl":
+                t = keep.tile([P, PACK, K_LID], BF16, name="zl%d" % g)
+                src = z_lid[g * GROUP : (g + 1) * GROUP, :].rearrange("(p t) k -> p t k", t=PACK)
+            else:
+                t = keep.tile([P, 2, K_CAM], BF16, name="zc%d%d" % key[1:])
+                src = z_cam[g * GROUP : (g + 1) * GROUP, :].rearrange("(p t) k -> p t k", t=PACK)[:, 2 * key[2] : 2 * key[2] + 2, :]
+            nc.sync.dma_start(out=t[:], in_=src)
+            raw[key] = t
+
+        def load_half(key, src, row0, h):
+            t = keep.tile([P, PACK, HALF], BF16, name="%s%d%d" % key)
+            nc.sync.dma_start(
+                out=t[:], in_=src[row0 : row0 + GROUP, h * HALF : (h + 1) * HALF].rearrange("(p t) n -> p t n", t=PACK)
+            )
+            raw[key] = t
+
+        lam_rows = keep.tile([P, GROUP], BF16, name="lam_rows")
+        lam_wide = keep.tile([P, GROUP], F32, name="lam_wide")
+        lam = keep.tile([P, PACK, 2 * GROUPS], F32, name="lam")
+        nc.scalar.dma_start(out=lam_rows[0:GROUPS, :], in_=lam_cam.rearrange("(g s) -> g s", g=GROUPS))
+        nc.scalar.dma_start(out=lam_rows[GROUPS : 2 * GROUPS, :], in_=lam_lid.rearrange("(g s) -> g s", g=GROUPS))
+        nc.vector.memset(lam_wide[:], 0.0)
+
+        order = [parse(w) for w in LOADS.split()]
+        for key in order:
+            if key[0] == "eta":
+                load_half(key, eta_pred, key[1] * GROUP, key[2])
+            elif key[0] == "hl":
+                load_half(key, h_lid, 0, key[2])
+            elif key[0] == "hc":
+                load_half(key, h_cam, key[1] * GROUP, key[2])
+            else:
+                load_z(key)
+
+        nc.vector.tensor_copy(out=lam_wide[0 : 2 * GROUPS, :], in_=lam_rows[0 : 2 * GROUPS, :])
+
+        def turn_lam():
+            bank = psum.tile([P, PACK, P], F32, name="acc", bufs=ACC)
+            for t in range(PACK):
+                nc.tensor.transpose(bank[:, t, :], lam_wide[:, t:GROUP:PACK], ident[:])
+            nc.scalar.copy(out=lam[:], in_=bank[:, :, 0 : 2 * GROUPS])
+
+        grouped = {}
+        codes = {}
+
+        def quantize(key, bufs_tag):
+            words = ring.tile([P, GROUP], U32, name="w_" + bufs_tag[0], bufs=bufs_tag[1], align_bytes=64)
+            scales = ring.tile([P, GROUP], U8, name="s_" + bufs_tag[0], bufs=bufs_tag[1], align_bytes=64)
+            nc.vector.quantize_mx(out=words[:].bitcast(FP8X4), scales=scales[:], in_=grouped[key][:])
+            codes[key] = (words, scales)
+
+        def interleave_h(key, engine, c0=0, c1=HALF):
+            if key not in grouped:
+                grouped[key] = ring.tile([P, PACK * HALF], BF16, name="h_grouped", bufs=2, align_bytes=64)
+            engine(
+                out=grouped[key][:].rearrange("p (c i t) -> p c t i", i=4, t=PACK)[:, c0 // 4 : c1 // 4],
+                in_=raw[key][:].rearrange("p t (c i) -> p c t i", i=4)[:, c0 // 4 : c1 // 4],
+            )
+
+        def turn_z(key, pieces):
+            dst = ring.tile([P, PACK * GROUP], BF16, name="z_grouped", bufs=3, align_bytes=64)
+            dst_words = dst[:].bitcast(F32).rearrange("p (b j r u) -> p b j r u", b=2, j=2, u=2)
+            banks = []
+            for b in range(2):
+                bank = psum.tile([P, 2, 2, P], F32, name="turn", bufs=8 - ACC)
+                for j in range(2):
+                    src, t, c = pieces[2 * b + j]
+                    words = src[:, t, :].bitcast(F32)
+                    for u in range(2):
+                        nc.tensor.transpose(bank[:, j, u, :], words[:, 256 * c + u : 256 * (c + 1) : 2], ident[:])
+                banks.append(bank)
+            for b in range(2):
+                nc.scalar.copy(out=dst_words[:, b], in_=banks[b][:].rearrange("p j u r -> p j r u"))
+            grouped[key] = dst
+
+        ys = {}
+        y_scales = keep.tile([P, N], U8, name="y_scales", align_bytes=64)
+
+        def lid_tile(i):
+            unit, t = divmod(i, PACK)
+            g, n0, width = UNITS[unit]
+            h = n0 // HALF
+            n = slice(n0 % HALF, n0 % HALF + width)
+            if t == 0:
+                ys[unit] = keep.tile([P, PACK, width], F32, name="y%d" % unit)
+            zw, zs = codes["zl", g]
+            hw, hs = codes["hl", 0, h]
+            acc = psum.tile([P, width], F32, name="acc", bufs=ACC)
+            cols = slice(t * P, (t + 1) * P)
+            nc.tensor.matmul_mx(
+                out=acc[:], lhsT=zw[:, cols].bitcast(FP8X4), lhsT_scale=zs[:, cols],
+                rhs=hw[:, n].bitcast(FP8X4), rhs_scale=hs[:, n], start=True, stop=True,
+            )
+            y = ys[unit][:, t, :]
+            eta = raw["eta", g, h][:, t, n]
+            factor = lam[:, t, GROUPS + g : GROUPS + g + 1]
+            if i in ASSIST:
+                nc.scalar.activation(out=y, in_=acc[:], func=ACT.Copy, scale=factor)
+                for c0 in range(0, width, GADD):
+                    nc.gpsimd.tensor_tensor(out=y[:, c0 : c0 + GADD], in0=y[:, c0 : c0 + GADD], in1=eta[:, c0 : c0 + GADD], op=ALU.add)
+            else:
+                nc.vector.scalar_tensor_tensor(out=y, in0=acc[:], scalar=factor, in1=eta, op0=ALU.mult, op1=ALU.add)
+
+        def cam_tile(i):
+            unit, t = divmod(i, PACK)
+            g, n0, width = UNITS[unit]
+            h = n0 // HALF
+            n = slice(n0 % HALF, n0 % HALF + width)
+            zw, zs = codes["zc", g, t // 2]
+            acc = psum.tile([P, width], F32, name="acc", bufs=ACC)
+            for c in range(CAM_PASSES):
+                hw, hs = codes["hc", c, h]
+                j = 2 * (t % 2) + c
+                cols = slice(j * P, (j + 1) * P)
+                nc.tensor.matmul_mx(
+                    out=acc[:], lhsT=zw[:, cols].bitcast(FP8X4), lhsT_scale=zs[:, cols],
+                    rhs=hw[:, n].bitcast(FP8X4), rhs_scale=hs[:, n], start=(c == 0), stop=(c == CAM_PASSES - 1),
+                )
+            y = ys[unit][:, t, :]
+            nc.vector.scalar_tensor_tensor(
+                out=y, in0=acc[:], scalar=lam[:, t, g : g + 1], in1=y, op0=ALU.mult, op1=ALU.add
+            )
+
+        def store_y(unit, t0, t1):
+            g, n0, width = UNITS[unit]
+            rows = out_0[g * GROUP : (g + 1) * GROUP, n0 : n0 + width].rearrange("(p t) n -> p t n", t=PACK)
+            nc.sync.dma_start(out=rows[:, t0:t1, :], in_=ys[unit][:, t0:t1, :])
+
+        rounded = {}
+
+        def round_y(unit, c0, c1, engine):
+            if unit not in rounded:
+                rounded[unit] = ring.tile([P, PACK * UNITS[unit][2]], BF16, name="rounded", bufs=2, align_bytes=64)
+            d = rounded[unit][:].rearrange("p (c i t) -> p c t i", i=4, t=PACK)
+            s = ys[unit][:].rearrange("p t (c i) -> p c t i", i=4)
+            engine(out=d[:, c0 // 4 : c1 // 4], in_=s[:, c0 // 4 : c1 // 4])
+
+        def plane_y(unit):
+            g, n0, width = UNITS[unit]
+            cols = slice(n0, n0 + width)
+            words = ring.tile([P, width], U32, name="y_words", bufs=3, align_bytes=64)
+            nc.vector.quantize_mx(out=words[:].bitcast(FP8X4), scales=y_scales[PACK * g : P, cols], in_=rounded[unit][:])
+            nc.sync.dma_start(
+                out=out_1[g].rearrange("p m t -> p (m t)").bitcast(I32)[:, cols], in_=words[:].bitcast(I32)
+            )
+
+        def store_scales(c0, c1, queues):
+            for q in range(4):
+                queues[q].dma_start(
+                    out=out_2.bitcast(I32)[:, 4 * q : 4 * q + 4, c0 // 4 : c1 // 4],
+                    in_=y_scales[32 * q : 32 * q + 16, c0:c1].bitcast(I32),
+                )
+
+        def interleave_on_gpsimd(out, in_):
+            for c0 in range(0, out.shape[1], GPART):
+                nc.gpsimd.tensor_scalar(
+                    out=out[:, c0 : c0 + GPART], in0=in_[:, c0 : c0 + GPART],
+                    scalar1=1.0, scalar2=0.0, op0=ALU.mult, op1=ALU.add,
+                )
+
+        def interleave_shared(out, in_):
+            nc.scalar.copy(out=out[:, 0:SPLIT], in_=in_[:, 0:SPLIT])
+            nc.vector.tensor_copy(out=out[:, SPLIT:128], in_=in_[:, SPLIT:128])
+
+        engines = {"V": nc.vector.tensor_copy, "S": nc.scalar.copy, "G": interleave_on_gpsimd, "B": interleave_shared}
+        for word in PLAN.split():
+            op, arg = word[0], word[1:]
+            if op == "L":
+                lid_tile(int(arg))
+            elif op == "C":
+                cam_tile(int(arg))
+                if int(arg) % PACK == PACK - 1:
+                    store_y(int(arg) // PACK, 0, PACK)
+            elif op == "c":
+                cam_tile(int(arg))
+                if int(arg) % 2 == 1:
+                    store_y(int(arg) // PACK, int(arg) % PACK - 1, int(arg) % PACK + 1)
+            elif op == "I":
+                k, c0, c1, e = arg.split(":")
+                interleave_h(parse(k), engines[e], int(c0), int(c1))
+            elif op == "M":
+                turn_lam()
+            elif op == "R":
+                u, c0, c1, e = arg.split(":")
+                round_y(int(u), int(c0), int(c1), engines[e])
+            elif op == "Y":
+                w = [int(x) for x in arg.split(":")]
+                plane_y(*w)
+            elif op == "Z":
+                c0, c1, qs = arg.split(":")
+                store_scales(int(c0), int(c1), [{"s": nc.sync, "a": nc.scalar, "g": nc.gpsimd}[x] for x in qs])
+            elif op == "T":
+                key = parse(arg)
+                turn_z(key, [(raw[key], t, 0) for t in range(PACK)] if key[0] == "zl" else [(raw[key], j // 2, j % 2) for j in range(4)])
+            elif op == "Q":
+                key = parse(arg)
+                quantize(key, {"hl": ("h", 6), "hc": ("h", 6), "zl": ("zl", 2), "zc": ("zc", 4)}[key[0]])
+            else:
+                interleave_h(parse(arg), engines[op])

@@ -17,33 +17,27 @@ ACT = mybir.ActivationFunctionType
 
 P = 128
 PACK = 4
-GROUP = P * PACK
-GROUPS = M // GROUP
+STRETCH = P * PACK
+GROUPS = M // STRETCH
+CAM_PASSES = K_CAM // STRETCH
 HALF = 512
-HALVES = N // HALF
-CAM_PASSES = K_CAM // GROUP
-TILES = GROUPS * HALVES * PACK
+QUARTER = HALF // 2
+RUN = 4
+QUADRANTS = 4
 
-UNITS = [(0, 0, 512), (1, 0, 512), (0, 512, 512), (1, 512, 512), (2, 0, 512), (2, 512, 512), (3, 0, 512), (3, 512, 256), (3, 768, 256)]
-LEAD = 4
-TURN_AHEAD = 8
-QUANT_AHEAD = 2
-H_AHEAD = 10
-PLANE_LAG = 8
-ASSIST = ()
-ASSIST_FROM = 1
-H_ENG = "VSVSSS"
-SPLIT = 44
-ACC = 6
-GADD = 512
-GPART = 32
-LOADS = "hl00 zl0 hc00 eta00 hc10 zc00 zc01 zl1 eta10 zc10 zc11 hl01 eta01 hc01 hc11 eta11 zl2 eta20 zc20 zc21 eta21 zl3 eta30 zc30 zc31 eta31"
-PLAN = "Vhl00 Tzl0 M Qhl00 Vhc00 Qzl0 Qhc00 L0 L1 L2 L3 Ihc10:0:304:S Tzc00 Ihc10:304:512:V Tzc01 Qzc00 Qhc10 C0 Qzc01 Tzl1 C1 C2 Qzl1 C3 Tzc10 L4 L5 Tzc11 Qzc10 L6 Shl01 L7 C4 Qzc11 C5 Shc01 C6 Qhl01 C7 Shc11 L8 L9 Qhc01 L10 Tzl2 L11 L12 Qhc11 L13 Tzc20 R0:0:256:S L14 C8 R0:256:512:S Qzl2 L15 C9 R1:0:256:S C10 Y0 Tzc21 R1:256:512:S C11 Qzc20 C12 R2:0:256:S C13 Y1 R2:256:512:S C14 Qzc21 L16 C15 Y2 Tzl3 R3:0:256:S R3:256:512:S L17 C16 L18 C17 L19 C18 Y3 Tzc30 Qzl3 L20 C19 L21 C20 Tzc31 R4:0:256:S R4:256:512:S L22 C21 Qzc30 L23 C22 Qzc31 L24 C23 R5:0:256:S R5:256:512:S Y4 L25 C24 L26 C25 L27 C26 Y5 L28 C27 R6:0:256:S R6:256:512:S L29 C28 L30 C29 L31 C30 L32 C31 L33 R7:0:256:S L34 c32 L35 c33 Y6 Z0:512:ssss c34 c35 R8:0:84:S Y7 R8:84:256:V Y8 Z512:1024:aass"
+SPANS = [(g, n0, HALF) for g in range(GROUPS) for n0 in (0, HALF)][:-1]
+SPANS = SPANS + [(GROUPS - 1, HALF, QUARTER), (GROUPS - 1, HALF + QUARTER, QUARTER)]
+PAIRS = 2 * len(SPANS)
+PAIRS_PER_GROUP = 4
+
+ACC_BANKS = 6
+TURN_BANKS = 2
 
 
-def parse(word):
-    n = 3 if word.startswith("eta") else 2
-    return (word[:n],) + tuple(int(c) for c in word[n:])
+def is_shared(tile):
+    pair = tile // 2
+    turning = pair < PAIRS_PER_GROUP * (GROUPS - 1)
+    return tile % 2 == 0 and PAIRS_PER_GROUP <= pair < PAIRS - 1 and not (turning and pair % PAIRS_PER_GROUP == 2)
 
 
 def tile_camera_lidar_information_fusion_g2_kernel(
@@ -59,206 +53,242 @@ def tile_camera_lidar_information_fusion_g2_kernel(
         ident = keep.tile([P, P], F32, name="ident")
         make_identity(nc, ident[:])
 
-        raw = {}
-
-        def load_z(key):
-            g = key[1]
-            if key[0] == "zl":
-                t = keep.tile([P, PACK, K_LID], BF16, name="zl%d" % g)
-                src = z_lid[g * GROUP : (g + 1) * GROUP, :].rearrange("(p t) k -> p t k", t=PACK)
-            else:
-                t = keep.tile([P, 2, K_CAM], BF16, name="zc%d%d" % key[1:])
-                src = z_cam[g * GROUP : (g + 1) * GROUP, :].rearrange("(p t) k -> p t k", t=PACK)[:, 2 * key[2] : 2 * key[2] + 2, :]
-            nc.sync.dma_start(out=t[:], in_=src)
-            raw[key] = t
-
-        def load_half(key, src, row0, h):
-            t = keep.tile([P, PACK, HALF], BF16, name="%s%d%d" % key)
-            nc.sync.dma_start(
-                out=t[:], in_=src[row0 : row0 + GROUP, h * HALF : (h + 1) * HALF].rearrange("(p t) n -> p t n", t=PACK)
-            )
-            raw[key] = t
-
-        lam_rows = keep.tile([P, GROUP], BF16, name="lam_rows")
-        lam_wide = keep.tile([P, GROUP], F32, name="lam_wide")
+        lam_rows = keep.tile([P, STRETCH], BF16, name="lam_rows")
+        lam_sorted = keep.tile([P, PACK, P], F32, name="lam_sorted")
         lam = keep.tile([P, PACK, 2 * GROUPS], F32, name="lam")
         nc.scalar.dma_start(out=lam_rows[0:GROUPS, :], in_=lam_cam.rearrange("(g s) -> g s", g=GROUPS))
         nc.scalar.dma_start(out=lam_rows[GROUPS : 2 * GROUPS, :], in_=lam_lid.rearrange("(g s) -> g s", g=GROUPS))
-        nc.vector.memset(lam_wide[:], 0.0)
+        nc.vector.memset(lam_sorted[:], 0.0)
 
-        order = [parse(w) for w in LOADS.split()]
-        for key in order:
-            if key[0] == "eta":
-                load_half(key, eta_pred, key[1] * GROUP, key[2])
-            elif key[0] == "hl":
-                load_half(key, h_lid, 0, key[2])
-            elif key[0] == "hc":
-                load_half(key, h_cam, key[1] * GROUP, key[2])
-            else:
-                load_z(key)
+        raw = {}
 
-        nc.vector.tensor_copy(out=lam_wide[0 : 2 * GROUPS, :], in_=lam_rows[0 : 2 * GROUPS, :])
+        def load(key):
+            kind = key[0]
+            source = {"z_lid": z_lid, "z_cam": z_cam, "h_lid": h_lid, "h_cam": h_cam, "eta": eta_pred}[kind]
+            rows = source[key[1] * STRETCH : (key[1] + 1) * STRETCH, :].rearrange("(p t) n -> p t n", t=PACK)
+            if kind == "z_cam":
+                rows = rows[:, 2 * key[2] : 2 * key[2] + 2, :]
+            elif kind != "z_lid":
+                rows = rows[:, :, key[2] * HALF : (key[2] + 1) * HALF]
+            piece = keep.tile(list(rows.shape), BF16, name="_".join(str(part) for part in key))
+            nc.sync.dma_start(out=piece[:], in_=rows)
+            raw[key] = piece
+
+        first_span = [("z_lid", 0), ("h_lid", 0, 0), ("z_cam", 0, 0), ("h_cam", 0, 0), ("h_cam", 1, 0), ("eta", 0, 0),
+                      ("z_cam", 0, 1)]
+        second_span = [("h_lid", 0, 1), ("z_lid", 1), ("h_cam", 0, 1), ("z_cam", 1, 0), ("h_cam", 1, 1), ("eta", 0, 1)]
+        for key in first_span + second_span:
+            load(key)
+        for g in range(1, GROUPS):
+            if g > 1:
+                load(("z_cam", g, 0))
+            load(("z_cam", g, 1))
+            if g + 1 < GROUPS:
+                load(("z_lid", g + 1))
+            load(("eta", g, 0))
+            load(("eta", g, 1))
+
+        nc.scalar.activation(
+            out=lam_sorted[0 : 2 * GROUPS],
+            in_=lam_rows[0 : 2 * GROUPS, :].rearrange("r (p t) -> r t p", t=PACK),
+            func=ACT.Copy,
+        )
 
         def turn_lam():
-            bank = psum.tile([P, PACK, P], F32, name="acc", bufs=ACC)
+            bank = psum.tile([P, PACK, P], F32, name="acc", bufs=ACC_BANKS)
             for t in range(PACK):
-                nc.tensor.transpose(bank[:, t, :], lam_wide[:, t:GROUP:PACK], ident[:])
+                nc.tensor.transpose(bank[:, t, :], lam_sorted[:, t, :], ident[:])
             nc.scalar.copy(out=lam[:], in_=bank[:, :, 0 : 2 * GROUPS])
+
+        def interleave(copy, dst, src, c0, c1):
+            copy(
+                out=dst[:].rearrange("p (c i t) -> p c t i", i=RUN, t=PACK)[:, c0 // RUN : c1 // RUN],
+                in_=src[:].rearrange("p t (c i) -> p c t i", i=RUN)[:, c0 // RUN : c1 // RUN],
+            )
 
         grouped = {}
         codes = {}
 
-        def quantize(key, bufs_tag):
-            words = ring.tile([P, GROUP], U32, name="w_" + bufs_tag[0], bufs=bufs_tag[1], align_bytes=64)
-            scales = ring.tile([P, GROUP], U8, name="s_" + bufs_tag[0], bufs=bufs_tag[1], align_bytes=64)
-            nc.vector.quantize_mx(out=words[:].bitcast(FP8X4), scales=scales[:], in_=grouped[key][:])
-            codes[key] = (words, scales)
-
-        def interleave_h(key, engine, c0=0, c1=HALF):
+        def interleave_h(key, copy, c0=0, c1=HALF):
             if key not in grouped:
                 grouped[key] = ring.tile([P, PACK * HALF], BF16, name="h_grouped", bufs=2, align_bytes=64)
-            engine(
-                out=grouped[key][:].rearrange("p (c i t) -> p c t i", i=4, t=PACK)[:, c0 // 4 : c1 // 4],
-                in_=raw[key][:].rearrange("p t (c i) -> p c t i", i=4)[:, c0 // 4 : c1 // 4],
-            )
+            interleave(copy, grouped[key], raw[key], c0, c1)
 
-        def turn_z(key, pieces):
-            dst = ring.tile([P, PACK * GROUP], BF16, name="z_grouped", bufs=3, align_bytes=64)
-            dst_words = dst[:].bitcast(F32).rearrange("p (b j r u) -> p b j r u", b=2, j=2, u=2)
+        def turn_z(key):
+            dst = ring.tile([P, PACK * STRETCH], BF16, name="z_grouped", bufs=3, align_bytes=64)
+            dst_words = dst[:].bitcast(F32).rearrange("p (b j r u) -> p b j r u", b=TURN_BANKS, j=2, u=2)
+            src_words = raw[key][:].rearrange("p t k -> p (t k)").bitcast(F32)
             banks = []
-            for b in range(2):
-                bank = psum.tile([P, 2, 2, P], F32, name="turn", bufs=8 - ACC)
+            for b in range(TURN_BANKS):
+                bank = psum.tile([P, 2, 2, P], F32, name="turn", bufs=TURN_BANKS)
                 for j in range(2):
-                    src, t, c = pieces[2 * b + j]
-                    words = src[:, t, :].bitcast(F32)
+                    first = (2 * b + j) * 2 * P
                     for u in range(2):
-                        nc.tensor.transpose(bank[:, j, u, :], words[:, 256 * c + u : 256 * (c + 1) : 2], ident[:])
+                        nc.tensor.transpose(bank[:, j, u, :], src_words[:, first + u : first + 2 * P : 2], ident[:])
                 banks.append(bank)
-            for b in range(2):
+            for b in range(TURN_BANKS):
                 nc.scalar.copy(out=dst_words[:, b], in_=banks[b][:].rearrange("p j u r -> p j r u"))
             grouped[key] = dst
 
-        ys = {}
-        y_scales = keep.tile([P, N], U8, name="y_scales", align_bytes=64)
+        code_bufs = {"h": 2 * (1 + CAM_PASSES), "z_lid": 2, "z_cam": 4}
 
-        def lid_tile(i):
-            unit, t = divmod(i, PACK)
-            g, n0, width = UNITS[unit]
-            h = n0 // HALF
-            n = slice(n0 % HALF, n0 % HALF + width)
-            if t == 0:
-                ys[unit] = keep.tile([P, PACK, width], F32, name="y%d" % unit)
-            zw, zs = codes["zl", g]
-            hw, hs = codes["hl", 0, h]
-            acc = psum.tile([P, width], F32, name="acc", bufs=ACC)
-            cols = slice(t * P, (t + 1) * P)
-            nc.tensor.matmul_mx(
-                out=acc[:], lhsT=zw[:, cols].bitcast(FP8X4), lhsT_scale=zs[:, cols],
-                rhs=hw[:, n].bitcast(FP8X4), rhs_scale=hs[:, n], start=True, stop=True,
-            )
-            y = ys[unit][:, t, :]
-            eta = raw["eta", g, h][:, t, n]
-            factor = lam[:, t, GROUPS + g : GROUPS + g + 1]
-            if i in ASSIST:
-                nc.scalar.activation(out=y, in_=acc[:], func=ACT.Copy, scale=factor)
-                for c0 in range(0, width, GADD):
-                    nc.gpsimd.tensor_tensor(out=y[:, c0 : c0 + GADD], in0=y[:, c0 : c0 + GADD], in1=eta[:, c0 : c0 + GADD], op=ALU.add)
-            else:
-                nc.vector.scalar_tensor_tensor(out=y, in0=acc[:], scalar=factor, in1=eta, op0=ALU.mult, op1=ALU.add)
+        def quantize(key):
+            tag = "h" if key[0].startswith("h") else key[0]
+            words = ring.tile([P, STRETCH], U32, name="words_" + tag, bufs=code_bufs[tag], align_bytes=64)
+            scales = ring.tile([P, STRETCH], U8, name="scales_" + tag, bufs=code_bufs[tag], align_bytes=64)
+            nc.vector.quantize_mx(out=words[:].bitcast(FP8X4), scales=scales[:], in_=grouped[key][:])
+            codes[key] = (words, scales)
 
-        def cam_tile(i):
-            unit, t = divmod(i, PACK)
-            g, n0, width = UNITS[unit]
-            h = n0 // HALF
-            n = slice(n0 % HALF, n0 % HALF + width)
-            zw, zs = codes["zc", g, t // 2]
-            acc = psum.tile([P, width], F32, name="acc", bufs=ACC)
-            for c in range(CAM_PASSES):
-                hw, hs = codes["hc", c, h]
-                j = 2 * (t % 2) + c
-                cols = slice(j * P, (j + 1) * P)
+        def product(width, passes):
+            acc = psum.tile([P, width], F32, name="acc", bufs=ACC_BANKS)
+            for c, (z_key, j, h_key, columns) in enumerate(passes):
+                z_words, z_scales = codes[z_key]
+                h_words, h_scales = codes[h_key]
+                samples = slice(j * P, (j + 1) * P)
                 nc.tensor.matmul_mx(
-                    out=acc[:], lhsT=zw[:, cols].bitcast(FP8X4), lhsT_scale=zs[:, cols],
-                    rhs=hw[:, n].bitcast(FP8X4), rhs_scale=hs[:, n], start=(c == 0), stop=(c == CAM_PASSES - 1),
+                    out=acc[:],
+                    lhsT=z_words[:, samples].bitcast(FP8X4),
+                    lhsT_scale=z_scales[:, samples],
+                    rhs=h_words[:, columns].bitcast(FP8X4),
+                    rhs_scale=h_scales[:, columns],
+                    start=(c == 0),
+                    stop=(c == len(passes) - 1),
                 )
-            y = ys[unit][:, t, :]
+            return acc
+
+        ys = {}
+
+        def place(tile):
+            span, t = divmod(tile, PACK)
+            g, n0, width = SPANS[span]
+            return span, t, g, n0 // HALF, slice(n0 % HALF, n0 % HALF + width), width
+
+        def lidar(tile):
+            span, t, g, half, columns, width = place(tile)
+            if span not in ys:
+                ys[span] = keep.tile([P, PACK, width], F32, name="y%d" % span)
+            acc = product(width, [(("z_lid", g), t, ("h_lid", 0, half), columns)])
+            y = ys[span][:, t, :]
+            factor = lam[:, t, GROUPS + g : GROUPS + g + 1]
+            if is_shared(tile):
+                nc.scalar.activation(out=y, in_=acc[:], func=ACT.Copy, scale=factor)
+            else:
+                nc.vector.scalar_tensor_tensor(
+                    out=y, in0=acc[:], scalar=factor, in1=raw["eta", g, half][:, t, columns], op0=ALU.mult, op1=ALU.add
+                )
+
+        def camera(tile):
+            span, t, g, half, columns, width = place(tile)
+            acc = product(
+                width,
+                [(("z_cam", g, t // 2), 2 * (t % 2) + c, ("h_cam", c, half), columns) for c in range(CAM_PASSES)],
+            )
+            y = ys[span][:, t, :]
             nc.vector.scalar_tensor_tensor(
                 out=y, in0=acc[:], scalar=lam[:, t, g : g + 1], in1=y, op0=ALU.mult, op1=ALU.add
             )
-
-        def store_y(unit, t0, t1):
-            g, n0, width = UNITS[unit]
-            rows = out_0[g * GROUP : (g + 1) * GROUP, n0 : n0 + width].rearrange("(p t) n -> p t n", t=PACK)
-            nc.sync.dma_start(out=rows[:, t0:t1, :], in_=ys[unit][:, t0:t1, :])
+            if is_shared(tile):
+                nc.gpsimd.tensor_tensor(out=y, in0=y, in1=raw["eta", g, half][:, t, columns], op=ALU.add)
+            if t % 2 == 1:
+                n0 = SPANS[span][1]
+                rows = out_0[g * STRETCH : (g + 1) * STRETCH, n0 : n0 + width].rearrange("(p t) n -> p t n", t=PACK)
+                nc.sync.dma_start(out=rows[:, t - 1 : t + 1, :], in_=ys[span][:, t - 1 : t + 1, :])
 
         rounded = {}
 
-        def round_y(unit, c0, c1, engine):
-            if unit not in rounded:
-                rounded[unit] = ring.tile([P, PACK * UNITS[unit][2]], BF16, name="rounded", bufs=2, align_bytes=64)
-            d = rounded[unit][:].rearrange("p (c i t) -> p c t i", i=4, t=PACK)
-            s = ys[unit][:].rearrange("p t (c i) -> p c t i", i=4)
-            engine(out=d[:, c0 // 4 : c1 // 4], in_=s[:, c0 // 4 : c1 // 4])
+        def round_y(span, copy, c0, c1):
+            if span not in rounded:
+                rounded[span] = ring.tile([P, PACK * SPANS[span][2]], BF16, name="rounded", bufs=2, align_bytes=64)
+            interleave(copy, rounded[span], ys[span], c0, c1)
 
-        def plane_y(unit):
-            g, n0, width = UNITS[unit]
-            cols = slice(n0, n0 + width)
-            words = ring.tile([P, width], U32, name="y_words", bufs=3, align_bytes=64)
-            nc.vector.quantize_mx(out=words[:].bitcast(FP8X4), scales=y_scales[PACK * g : P, cols], in_=rounded[unit][:])
+        y_scales = keep.tile([P, N], U8, name="y_scales", align_bytes=64)
+
+        def quantize_y(span):
+            g, n0, width = SPANS[span]
+            columns = slice(n0, n0 + width)
+            words = ring.tile([P, width], U32, name="words_y", bufs=3, align_bytes=64)
+            nc.vector.quantize_mx(
+                out=words[:].bitcast(FP8X4), scales=y_scales[PACK * g : P, columns], in_=rounded[span][:]
+            )
             nc.sync.dma_start(
-                out=out_1[g].rearrange("p m t -> p (m t)").bitcast(I32)[:, cols], in_=words[:].bitcast(I32)
+                out=out_1[g].rearrange("p m t -> p (m t)").bitcast(I32)[:, columns], in_=words[:].bitcast(I32)
             )
 
-        def store_scales(c0, c1, queues):
-            for q in range(4):
-                queues[q].dma_start(
-                    out=out_2.bitcast(I32)[:, 4 * q : 4 * q + 4, c0 // 4 : c1 // 4],
-                    in_=y_scales[32 * q : 32 * q + 16, c0:c1].bitcast(I32),
+        def store_scales(g0, g1, queues):
+            for quad in range(QUADRANTS):
+                queues[quad].dma_start(
+                    out=out_2.bitcast(I32)[g0:g1, PACK * quad : PACK * quad + PACK, :],
+                    in_=y_scales[32 * quad + PACK * g0 : 32 * quad + PACK * g1, :].bitcast(I32),
                 )
 
-        def interleave_on_gpsimd(out, in_):
-            for c0 in range(0, out.shape[1], GPART):
-                nc.gpsimd.tensor_scalar(
-                    out=out[:, c0 : c0 + GPART], in0=in_[:, c0 : c0 + GPART],
-                    scalar1=1.0, scalar2=0.0, op0=ALU.mult, op1=ALU.add,
-                )
+        on_vector, on_scalar = nc.vector.tensor_copy, nc.scalar.copy
 
-        def interleave_shared(out, in_):
-            nc.scalar.copy(out=out[:, 0:SPLIT], in_=in_[:, 0:SPLIT])
-            nc.vector.tensor_copy(out=out[:, SPLIT:128], in_=in_[:, SPLIT:128])
+        turn_z(("z_lid", 0))
+        interleave_h(("h_lid", 0, 0), on_vector)
+        turn_z(("z_cam", 0, 0))
+        turn_lam()
+        quantize(("z_lid", 0))
+        quantize(("h_lid", 0, 0))
+        interleave_h(("h_cam", 0, 0), on_vector)
+        quantize(("z_cam", 0, 0))
+        interleave_h(("h_cam", 1, 0), on_scalar, 0, QUARTER)
+        interleave_h(("h_cam", 1, 0), on_vector, QUARTER, HALF)
+        quantize(("h_cam", 0, 0))
+        lidar(0)
+        quantize(("h_cam", 1, 0))
+        for tile in (1, 2, 3):
+            lidar(tile)
+        turn_z(("z_cam", 0, 1))
+        camera(0)
+        interleave_h(("h_lid", 0, 1), on_scalar)
+        quantize(("z_cam", 0, 1))
+        camera(1)
+        turn_z(("z_lid", 1))
+        interleave_h(("h_cam", 0, 1), on_scalar)
+        camera(2)
+        quantize(("h_lid", 0, 1))
+        camera(3)
+        quantize(("z_lid", 1))
+        lidar(4)
+        lidar(5)
+        turn_z(("z_cam", 1, 0))
+        interleave_h(("h_cam", 1, 1), on_scalar, 0, QUARTER)
+        interleave_h(("h_cam", 1, 1), on_vector, QUARTER, HALF)
+        quantize(("h_cam", 0, 1))
+        lidar(6)
+        quantize(("h_cam", 1, 1))
+        lidar(7)
+        lidar_done = 2 * PACK
 
-        engines = {"V": nc.vector.tensor_copy, "S": nc.scalar.copy, "G": interleave_on_gpsimd, "B": interleave_shared}
-        for word in PLAN.split():
-            op, arg = word[0], word[1:]
-            if op == "L":
-                lid_tile(int(arg))
-            elif op == "C":
-                cam_tile(int(arg))
-                if int(arg) % PACK == PACK - 1:
-                    store_y(int(arg) // PACK, 0, PACK)
-            elif op == "c":
-                cam_tile(int(arg))
-                if int(arg) % 2 == 1:
-                    store_y(int(arg) // PACK, int(arg) % PACK - 1, int(arg) % PACK + 1)
-            elif op == "I":
-                k, c0, c1, e = arg.split(":")
-                interleave_h(parse(k), engines[e], int(c0), int(c1))
-            elif op == "M":
-                turn_lam()
-            elif op == "R":
-                u, c0, c1, e = arg.split(":")
-                round_y(int(u), int(c0), int(c1), engines[e])
-            elif op == "Y":
-                w = [int(x) for x in arg.split(":")]
-                plane_y(*w)
-            elif op == "Z":
-                c0, c1, qs = arg.split(":")
-                store_scales(int(c0), int(c1), [{"s": nc.sync, "a": nc.scalar, "g": nc.gpsimd}[x] for x in qs])
-            elif op == "T":
-                key = parse(arg)
-                turn_z(key, [(raw[key], t, 0) for t in range(PACK)] if key[0] == "zl" else [(raw[key], j // 2, j % 2) for j in range(4)])
-            elif op == "Q":
-                key = parse(arg)
-                quantize(key, {"hl": ("h", 6), "hc": ("h", 6), "zl": ("zl", 2), "zc": ("zc", 4)}[key[0]])
-            else:
-                interleave_h(parse(arg), engines[op])
+        for pair in range(2, PAIRS):
+            g, step = divmod(pair, PAIRS_PER_GROUP)
+            span = pair // 2
+            if step == 1 and g + 1 < GROUPS:
+                quantize(("z_lid", g + 1))
+            if step >= 2 and g + 1 < GROUPS:
+                quantize(("z_cam", g + 1, step - 2))
+            if pair % 2 == 1 and span >= 2:
+                quantize_y(span - 2)
+                if span - 2 == len(SPANS) // 2 - 1:
+                    store_scales(0, GROUPS // 2, [nc.sync] * QUADRANTS)
+            if step in (1, 2) and g + 1 < GROUPS:
+                turn_z(("z_cam", g + 1, step - 1))
+            if step == 3 and g + 2 < GROUPS:
+                turn_z(("z_lid", g + 2))
+            ahead = [tile for tile in (2 * pair + 2, 2 * pair + 3) if lidar_done <= tile < 2 * PAIRS]
+            camera(2 * pair)
+            for tile in ahead[:1]:
+                lidar(tile)
+            c0 = QUARTER * (pair % 2)
+            if c0 < SPANS[span - 1][2]:
+                round_y(span - 1, on_scalar, c0, c0 + QUARTER)
+            for tile in ahead[1:]:
+                lidar(tile)
+            camera(2 * pair + 1)
+
+        last = len(SPANS) - 1
+        round_y(last, on_scalar, 0, QUARTER // 2)
+        quantize_y(last - 1)
+        round_y(last, on_vector, QUARTER // 2, QUARTER)
+        quantize_y(last)
+        store_scales(GROUPS // 2, GROUPS, [nc.scalar, nc.scalar, nc.sync, nc.sync])

@@ -22,7 +22,7 @@ GROUPS = M // STRETCH
 CAM_PASSES = K_CAM // STRETCH
 HALF = 512
 QUARTER = HALF // 2
-RUN = 4
+RUN_BYTES = 8
 QUADRANTS = 4
 
 SPANS = [(g, n0, HALF) for g in range(GROUPS) for n0 in (0, HALF)][:-1]
@@ -100,10 +100,11 @@ def tile_camera_lidar_information_fusion_g2_kernel(
                 nc.tensor.transpose(bank[:, t, :], lam_sorted[:, t, :], ident[:])
             nc.scalar.copy(out=lam[:], in_=bank[:, :, 0 : 2 * GROUPS])
 
-        def interleave(copy, dst, src, c0, c1):
+        def interleave(copy, dst, src, src_bytes, c0, c1):
+            run = RUN_BYTES // src_bytes
             copy(
-                out=dst[:].rearrange("p (c i t) -> p c t i", i=RUN, t=PACK)[:, c0 // RUN : c1 // RUN],
-                in_=src[:].rearrange("p t (c i) -> p c t i", i=RUN)[:, c0 // RUN : c1 // RUN],
+                out=dst[:].rearrange("p (c i t) -> p c t i", i=run, t=PACK)[:, c0 // run : c1 // run],
+                in_=src[:].rearrange("p t (c i) -> p c t i", i=run)[:, c0 // run : c1 // run],
             )
 
         grouped = {}
@@ -112,7 +113,7 @@ def tile_camera_lidar_information_fusion_g2_kernel(
         def interleave_h(key, copy, c0=0, c1=HALF):
             if key not in grouped:
                 grouped[key] = ring.tile([P, PACK * HALF], BF16, name="h_grouped", bufs=2, align_bytes=64)
-            interleave(copy, grouped[key], raw[key], c0, c1)
+            interleave(copy, grouped[key], raw[key], 2, c0, c1)
 
         def turn_z(key):
             dst = ring.tile([P, PACK * STRETCH], BF16, name="z_grouped", bufs=3, align_bytes=64)
@@ -134,8 +135,8 @@ def tile_camera_lidar_information_fusion_g2_kernel(
 
         def quantize(key):
             tag = "h" if key[0].startswith("h") else key[0]
-            words = ring.tile([P, STRETCH], U32, name="words_" + tag, bufs=code_bufs[tag], align_bytes=64)
-            scales = ring.tile([P, STRETCH], U8, name="scales_" + tag, bufs=code_bufs[tag], align_bytes=64)
+            words = ring.tile([P, STRETCH], U32, name="words_" + tag, bufs=code_bufs[tag], align_bytes=256)
+            scales = ring.tile([P, STRETCH], U8, name="scales_" + tag, bufs=code_bufs[tag], align_bytes=256)
             nc.vector.quantize_mx(out=words[:].bitcast(FP8X4), scales=scales[:], in_=grouped[key][:])
             codes[key] = (words, scales)
 
@@ -199,7 +200,7 @@ def tile_camera_lidar_information_fusion_g2_kernel(
         def round_y(span, copy, c0, c1):
             if span not in rounded:
                 rounded[span] = ring.tile([P, PACK * SPANS[span][2]], BF16, name="rounded", bufs=2, align_bytes=64)
-            interleave(copy, rounded[span], ys[span], c0, c1)
+            interleave(copy, rounded[span], ys[span], 4, c0, c1)
 
         y_scales = keep.tile([P, N], U8, name="y_scales", align_bytes=64)
 
@@ -258,9 +259,16 @@ def tile_camera_lidar_information_fusion_g2_kernel(
         lidar(6)
         quantize(("h_cam", 1, 1))
         lidar(7)
-        lidar_done = 2 * PACK
+        quantize(("z_cam", 1, 0))
+        turn_z(("z_cam", 1, 1))
+        lidar(8)
+        lidar(9)
+        camera(4)
+        round_y(0, on_scalar, 0, QUARTER)
+        camera(5)
+        first_pair, lidar_done = 3, 10
 
-        for pair in range(2, PAIRS):
+        for pair in range(first_pair, PAIRS):
             g, step = divmod(pair, PAIRS_PER_GROUP)
             span = pair // 2
             if step == 1 and g + 1 < GROUPS:

@@ -32,12 +32,12 @@ PAIRS_PER_GROUP = 4
 
 ACC_BANKS = 6
 TURN_BANKS = 2
+LONG_LEAD_PAIRS = 10
 
 
 def is_shared(tile):
     pair = tile // 2
-    turning = pair < PAIRS_PER_GROUP * (GROUPS - 1)
-    return tile % 2 == 0 and PAIRS_PER_GROUP <= pair < PAIRS - 1 and not (turning and pair % PAIRS_PER_GROUP == 2)
+    return tile % 2 == 0 and PAIRS_PER_GROUP <= pair < PAIRS - 1 and pair != LONG_LEAD_PAIRS
 
 
 def tile_camera_lidar_information_fusion_g2_kernel(
@@ -68,7 +68,7 @@ def tile_camera_lidar_information_fusion_g2_kernel(
             rows = source[key[1] * STRETCH : (key[1] + 1) * STRETCH, :].rearrange("(p t) n -> p t n", t=PACK)
             if kind == "z_cam":
                 rows = rows[:, 2 * key[2] : 2 * key[2] + 2, :]
-            elif kind != "z_lid":
+            elif len(key) == 3:
                 rows = rows[:, :, key[2] * HALF : (key[2] + 1) * HALF]
             piece = keep.tile(list(rows.shape), BF16, name="_".join(str(part) for part in key))
             nc.sync.dma_start(out=piece[:], in_=rows)
@@ -85,8 +85,7 @@ def tile_camera_lidar_information_fusion_g2_kernel(
             load(("z_cam", g, 1))
             if g + 1 < GROUPS:
                 load(("z_lid", g + 1))
-            load(("eta", g, 0))
-            load(("eta", g, 1))
+            load(("eta", g))
 
         nc.scalar.activation(
             out=lam_sorted[0 : 2 * GROUPS],
@@ -104,7 +103,7 @@ def tile_camera_lidar_information_fusion_g2_kernel(
             run = RUN_BYTES // src_bytes
             copy(
                 out=dst[:].rearrange("p (c i t) -> p c t i", i=run, t=PACK)[:, c0 // run : c1 // run],
-                in_=src[:].rearrange("p t (c i) -> p c t i", i=run)[:, c0 // run : c1 // run],
+                in_=src.rearrange("p t (c i) -> p c t i", i=run)[:, c0 // run : c1 // run],
             )
 
         grouped = {}
@@ -113,7 +112,7 @@ def tile_camera_lidar_information_fusion_g2_kernel(
         def interleave_h(key, copy, c0=0, c1=HALF):
             if key not in grouped:
                 grouped[key] = ring.tile([P, PACK * HALF], BF16, name="h_grouped", bufs=2, align_bytes=64)
-            interleave(copy, grouped[key], raw[key], 2, c0, c1)
+            interleave(copy, grouped[key], raw[key][:], 2, c0, c1)
 
         def turn_z(key):
             dst = ring.tile([P, PACK * STRETCH], BF16, name="z_grouped", bufs=3, align_bytes=64)
@@ -157,6 +156,11 @@ def tile_camera_lidar_information_fusion_g2_kernel(
                 )
             return acc
 
+        def eta(g, half, t, columns):
+            if g == 0:
+                return raw["eta", g, half][:, t, columns]
+            return raw["eta", g][:, t, half * HALF : (half + 1) * HALF][:, columns]
+
         ys = {}
 
         def place(tile):
@@ -175,7 +179,7 @@ def tile_camera_lidar_information_fusion_g2_kernel(
                 nc.scalar.activation(out=y, in_=acc[:], func=ACT.Copy, scale=factor)
             else:
                 nc.vector.scalar_tensor_tensor(
-                    out=y, in0=acc[:], scalar=factor, in1=raw["eta", g, half][:, t, columns], op0=ALU.mult, op1=ALU.add
+                    out=y, in0=acc[:], scalar=factor, in1=eta(g, half, t, columns), op0=ALU.mult, op1=ALU.add
                 )
 
         def camera(tile):
@@ -189,7 +193,7 @@ def tile_camera_lidar_information_fusion_g2_kernel(
                 out=y, in0=acc[:], scalar=lam[:, t, g : g + 1], in1=y, op0=ALU.mult, op1=ALU.add
             )
             if is_shared(tile):
-                nc.gpsimd.tensor_tensor(out=y, in0=y, in1=raw["eta", g, half][:, t, columns], op=ALU.add)
+                nc.gpsimd.tensor_tensor(out=y, in0=y, in1=eta(g, half, t, columns), op=ALU.add)
             if t % 2 == 1:
                 n0 = SPANS[span][1]
                 rows = out_0[g * STRETCH : (g + 1) * STRETCH, n0 : n0 + width].rearrange("(p t) n -> p t n", t=PACK)
@@ -200,7 +204,7 @@ def tile_camera_lidar_information_fusion_g2_kernel(
         def round_y(span, copy, c0, c1):
             if span not in rounded:
                 rounded[span] = ring.tile([P, PACK * SPANS[span][2]], BF16, name="rounded", bufs=2, align_bytes=64)
-            interleave(copy, rounded[span], ys[span], 4, c0, c1)
+            interleave(copy, rounded[span], ys[span][:], 4, c0, c1)
 
         y_scales = keep.tile([P, N], U8, name="y_scales", align_bytes=64)
 
@@ -228,8 +232,8 @@ def tile_camera_lidar_information_fusion_g2_kernel(
         interleave_h(("h_lid", 0, 0), on_vector)
         turn_z(("z_cam", 0, 0))
         turn_lam()
-        quantize(("z_lid", 0))
         quantize(("h_lid", 0, 0))
+        quantize(("z_lid", 0))
         interleave_h(("h_cam", 0, 0), on_vector)
         quantize(("z_cam", 0, 0))
         interleave_h(("h_cam", 1, 0), on_scalar, 0, QUARTER)
@@ -283,7 +287,9 @@ def tile_camera_lidar_information_fusion_g2_kernel(
                 turn_z(("z_cam", g + 1, step - 1))
             if step == 3 and g + 2 < GROUPS:
                 turn_z(("z_lid", g + 2))
-            ahead = [tile for tile in (2 * pair + 2, 2 * pair + 3) if lidar_done <= tile < 2 * PAIRS]
+            lead = 2 if pair < LONG_LEAD_PAIRS else 1
+            ahead = list(range(lidar_done, min(2 * (pair + lead + 1), 2 * PAIRS)))
+            lidar_done = lidar_done + len(ahead)
             camera(2 * pair)
             for tile in ahead[:1]:
                 lidar(tile)

from contextlib import ExitStack

import concourse.mybir as mybir
from concourse.masks import make_identity

M, N, K_CAM, K_LID = 2048, 1024, 1024, 512
FLOPS = 2 * M * N * (K_CAM + K_LID)

F32 = mybir.dt.float32
BF16 = mybir.dt.bfloat16
U32 = mybir.dt.uint32
I32 = mybir.dt.int32
U8 = mybir.dt.uint8
FP8X4 = mybir.dt.float8_e4m3fn_x4
ALU = mybir.AluOpType
ACT = mybir.ActivationFunctionType

P = 128
PACK = 4
STRETCH = P * PACK
GROUPS = M // STRETCH
CAM_PASSES = K_CAM // STRETCH
HALF = 512
QUARTER = HALF // 2
RUN_BYTES = 8
QUADRANTS = 4

SPANS = [(g, n0, HALF) for g in range(GROUPS) for n0 in (0, HALF)][:-1]
SPANS = SPANS + [(GROUPS - 1, HALF, QUARTER), (GROUPS - 1, HALF + QUARTER, QUARTER)]
PAIRS = 2 * len(SPANS)
PAIRS_PER_GROUP = 4

ACC_BANKS = 6
TURN_BANKS = 2
LONG_LEAD_PAIRS = 10


def is_shared(tile):
    pair = tile // 2
    return tile % 2 == 0 and PAIRS_PER_GROUP <= pair < PAIRS - 1 and pair != LONG_LEAD_PAIRS


def tile_camera_lidar_information_fusion_g2_kernel(
    tc, z_cam, h_cam, z_lid, h_lid, lam_cam, lam_lid, eta_pred, out_0, out_1, out_2
):
    nc = tc.nc
    with ExitStack() as ctx:
        keep = ctx.enter_context(tc.tile_pool(name="keep", bufs=1))
        ring = ctx.enter_context(tc.tile_pool(name="ring", bufs=2))
        psum = ctx.enter_context(tc.psum_pool(name="psum", bufs=1))
        ctx.enter_context(tc.manual_schedule())

        ident = keep.tile([P, P], F32, name="ident")
        make_identity(nc, ident[:])

        lam_rows = keep.tile([P, STRETCH], BF16, name="lam_rows")
        lam_sorted = keep.tile([P, PACK, P], F32, name="lam_sorted")
        lam = keep.tile([P, PACK, 2 * GROUPS], F32, name="lam")
        nc.scalar.dma_start(out=lam_rows[0:GROUPS, :], in_=lam_cam.rearrange("(g s) -> g s", g=GROUPS))
        nc.scalar.dma_start(out=lam_rows[GROUPS : 2 * GROUPS, :], in_=lam_lid.rearrange("(g s) -> g s", g=GROUPS))
        nc.vector.memset(lam_sorted[:], 0.0)

        raw = {}

        def load(key):
            kind = key[0]
            source = {"z_lid": z_lid, "z_cam": z_cam, "h_lid": h_lid, "h_cam": h_cam, "eta": eta_pred}[kind]
            rows = source[key[1] * STRETCH : (key[1] + 1) * STRETCH, :].rearrange("(p t) n -> p t n", t=PACK)
            if kind == "z_cam":
                rows = rows[:, 2 * key[2] : 2 * key[2] + 2, :]
            elif len(key) == 3:
                rows = rows[:, :, key[2] * HALF : (key[2] + 1) * HALF]
            piece = keep.tile(list(rows.shape), BF16, name="_".join(str(part) for part in key))
            nc.sync.dma_start(out=piece[:], in_=rows)
            raw[key] = piece

        first_span = [("z_lid", 0), ("h_lid", 0, 0), ("z_cam", 0, 0), ("h_cam", 0, 0), ("h_cam", 1, 0), ("eta", 0, 0),
                      ("z_cam", 0, 1)]
        second_span = [("h_lid", 0, 1), ("z_lid", 1), ("h_cam", 0, 1), ("z_cam", 1, 0), ("h_cam", 1, 1), ("eta", 0, 1)]
        for key in first_span + second_span:
            load(key)
        for g in range(1, GROUPS):
            if g > 1:
                load(("z_cam", g, 0))
            load(("z_cam", g, 1))
            if g + 1 < GROUPS:
                load(("z_lid", g + 1))
            load(("eta", g))

        nc.scalar.activation(
            out=lam_sorted[0 : 2 * GROUPS],
            in_=lam_rows[0 : 2 * GROUPS, :].rearrange("r (p t) -> r t p", t=PACK),
            func=ACT.Copy,
        )

        def turn_lam():
            bank = psum.tile([P, PACK, P], F32, name="acc", bufs=ACC_BANKS)
            for t in range(PACK):
                nc.tensor.transpose(bank[:, t, :], lam_sorted[:, t, :], ident[:])
            nc.scalar.copy(out=lam[:], in_=bank[:, :, 0 : 2 * GROUPS])

        def interleave(copy, dst, src, src_bytes, c0, c1):
            run = RUN_BYTES // src_bytes
            copy(
                out=dst[:].rearrange("p (c i t) -> p c t i", i=run, t=PACK)[:, c0 // run : c1 // run],
                in_=src.rearrange("p t (c i) -> p c t i", i=run)[:, c0 // run : c1 // run],
            )

        grouped = {}
        codes = {}

        def interleave_h(key, copy, c0=0, c1=HALF):
            if key not in grouped:
                grouped[key] = ring.tile([P, PACK * HALF], BF16, name="h_grouped", bufs=2, align_bytes=64)
            interleave(copy, grouped[key], raw[key][:], 2, c0, c1)

        def turn_z(key):
            dst = ring.tile([P, PACK * STRETCH], BF16, name="z_grouped", bufs=3, align_bytes=64)
            dst_words = dst[:].bitcast(F32).rearrange("p (b j r u) -> p b j r u", b=TURN_BANKS, j=2, u=2)
            src_words = raw[key][:].rearrange("p t k -> p (t k)").bitcast(F32)
            banks = []
            for b in range(TURN_BANKS):
                bank = psum.tile([P, 2, 2, P], F32, name="turn", bufs=TURN_BANKS)
                for j in range(2):
                    first = (2 * b + j) * 2 * P
                    for u in range(2):
                        nc.tensor.transpose(bank[:, j, u, :], src_words[:, first + u : first + 2 * P : 2], ident[:])
                banks.append(bank)
            for b in range(TURN_BANKS):
                nc.scalar.copy(out=dst_words[:, b], in_=banks[b][:].rearrange("p j u r -> p j r u"))
            grouped[key] = dst

        code_bufs = {"h": 2 * (1 + CAM_PASSES), "z_lid": 2, "z_cam": 4}

        def quantize(key):
            tag = "h" if key[0].startswith("h") else key[0]
            words = ring.tile([P, STRETCH], U32, name="words_" + tag, bufs=code_bufs[tag], align_bytes=256)
            scales = ring.tile([P, STRETCH], U8, name="scales_" + tag, bufs=code_bufs[tag], align_bytes=256)
            nc.vector.quantize_mx(out=words[:].bitcast(FP8X4), scales=scales[:], in_=grouped[key][:])
            codes[key] = (words, scales)

        def product(width, passes):
            acc = psum.tile([P, width], F32, name="acc", bufs=ACC_BANKS)
            for c, (z_key, j, h_key, columns) in enumerate(passes):
                z_words, z_scales = codes[z_key]
                h_words, h_scales = codes[h_key]
                samples = slice(j * P, (j + 1) * P)
                nc.tensor.matmul_mx(
                    out=acc[:],
                    lhsT=z_words[:, samples].bitcast(FP8X4),
                    lhsT_scale=z_scales[:, samples],
                    rhs=h_words[:, columns].bitcast(FP8X4),
                    rhs_scale=h_scales[:, columns],
                    start=(c == 0),
                    stop=(c == len(passes) - 1),
                )
            return acc

        def eta(g, half, t, columns):
            if g == 0:
                return raw["eta", g, half][:, t, columns]
            return raw["eta", g][:, t, half * HALF : (half + 1) * HALF][:, columns]

        ys = {}

        def place(tile):
            span, t = divmod(tile, PACK)
            g, n0, width = SPANS[span]
            return span, t, g, n0 // HALF, slice(n0 % HALF, n0 % HALF + width), width

        def lidar(tile):
            span, t, g, half, columns, width = place(tile)
            if span not in ys:
                ys[span] = keep.tile([P, PACK, width], F32, name="y%d" % span)
            acc = product(width, [(("z_lid", g), t, ("h_lid", 0, half), columns)])
            y = ys[span][:, t, :]
            factor = lam[:, t, GROUPS + g : GROUPS + g + 1]
            if is_shared(tile):
                nc.scalar.activation(out=y, in_=acc[:], func=ACT.Copy, scale=factor)
            else:
                nc.vector.scalar_tensor_tensor(
                    out=y, in0=acc[:], scalar=factor, in1=eta(g, half, t, columns), op0=ALU.mult, op1=ALU.add
                )

        def camera(tile):
            span, t, g, half, columns, width = place(tile)
            acc = product(
                width,
                [(("z_cam", g, t // 2), 2 * (t % 2) + c, ("h_cam", c, half), columns) for c in range(CAM_PASSES)],
            )
            y = ys[span][:, t, :]
            nc.vector.scalar_tensor_tensor(
                out=y, in0=acc[:], scalar=lam[:, t, g : g + 1], in1=y, op0=ALU.mult, op1=ALU.add
            )
            if is_shared(tile):
                nc.gpsimd.tensor_tensor(out=y, in0=y, in1=eta(g, half, t, columns), op=ALU.add)
            if t % 2 == 1:
                n0 = SPANS[span][1]
                rows = out_0[g * STRETCH : (g + 1) * STRETCH, n0 : n0 + width].rearrange("(p t) n -> p t n", t=PACK)
                nc.sync.dma_start(out=rows[:, t - 1 : t + 1, :], in_=ys[span][:, t - 1 : t + 1, :])

        rounded = {}

        def round_y(span, copy, c0, c1):
            if span not in rounded:
                rounded[span] = ring.tile([P, PACK * SPANS[span][2]], BF16, name="rounded", bufs=2, align_bytes=64)
            interleave(copy, rounded[span], ys[span][:], 4, c0, c1)

        y_scales = keep.tile([P, N], U8, name="y_scales", align_bytes=64)

        def quantize_y(span):
            g, n0, width = SPANS[span]
            columns = slice(n0, n0 + width)
            words = ring.tile([P, width], U32, name="words_y", bufs=3, align_bytes=64)
            nc.vector.quantize_mx(
                out=words[:].bitcast(FP8X4), scales=y_scales[PACK * g : P, columns], in_=rounded[span][:]
            )
            nc.sync.dma_start(
                out=out_1[g].rearrange("p m t -> p (m t)").bitcast(I32)[:, columns], in_=words[:].bitcast(I32)
            )

        def store_scales(g0, g1, queues):
            for quad in range(QUADRANTS):
                queues[quad].dma_start(
                    out=out_2.bitcast(I32)[g0:g1, PACK * quad : PACK * quad + PACK, :],
                    in_=y_scales[32 * quad + PACK * g0 : 32 * quad + PACK * g1, :].bitcast(I32),
                )

        on_vector, on_scalar = nc.vector.tensor_copy, nc.scalar.copy

        turn_z(("z_lid", 0))
        interleave_h(("h_lid", 0, 0), on_vector)
        turn_z(("z_cam", 0, 0))
        turn_lam()
        quantize(("h_lid", 0, 0))
        quantize(("z_lid", 0))
        interleave_h(("h_cam", 0, 0), on_vector)
        quantize(("z_cam", 0, 0))
        interleave_h(("h_cam", 1, 0), on_scalar, 0, QUARTER)
        interleave_h(("h_cam", 1, 0), on_vector, QUARTER, HALF)
        quantize(("h_cam", 0, 0))
        lidar(0)
        quantize(("h_cam", 1, 0))
        for tile in (1, 2, 3):
            lidar(tile)
        turn_z(("z_cam", 0, 1))
        camera(0)
        interleave_h(("h_lid", 0, 1), on_scalar)
        quantize(("z_cam", 0, 1))
        camera(1)
        turn_z(("z_lid", 1))
        interleave_h(("h_cam", 0, 1), on_scalar)
        camera(2)
        quantize(("h_lid", 0, 1))
        camera(3)
        quantize(("z_lid", 1))
        lidar(4)
        lidar(5)
        turn_z(("z_cam", 1, 0))
        interleave_h(("h_cam", 1, 1), on_scalar, 0, QUARTER)
        interleave_h(("h_cam", 1, 1), on_vector, QUARTER, HALF)
        quantize(("h_cam", 0, 1))
        lidar(6)
        quantize(("h_cam", 1, 1))
        lidar(7)
        quantize(("z_cam", 1, 0))
        turn_z(("z_cam", 1, 1))
        lidar(8)
        lidar(9)
        camera(4)
        round_y(0, on_scalar, 0, QUARTER)
        camera(5)
        first_pair, lidar_done = 3, 10

        for pair in range(first_pair, PAIRS):
            g, step = divmod(pair, PAIRS_PER_GROUP)
            span = pair // 2
            if step == 1 and g + 1 < GROUPS:
                quantize(("z_lid", g + 1))
            if step >= 2 and g + 1 < GROUPS:
                quantize(("z_cam", g + 1, step - 2))
            if pair % 2 == 1 and span >= 2:
                quantize_y(span - 2)
                if span - 2 == len(SPANS) // 2 - 1:
                    store_scales(0, GROUPS // 2, [nc.sync] * QUADRANTS)
            if step in (1, 2) and g + 1 < GROUPS:
                turn_z(("z_cam", g + 1, step - 1))
            if step == 3 and g + 2 < GROUPS:
                turn_z(("z_lid", g + 2))
            lead = 2 if pair < LONG_LEAD_PAIRS else 1
            ahead = list(range(lidar_done, min(2 * (pair + lead + 1), 2 * PAIRS)))
            lidar_done = lidar_done + len(ahead)
            camera(2 * pair)
            for tile in ahead[:1]:
                lidar(tile)
            c0 = QUARTER * (pair % 2)
            if c0 < SPANS[span - 1][2]:
                round_y(span - 1, on_scalar, c0, c0 + QUARTER)
            for tile in ahead[1:]:
                lidar(tile)
            camera(2 * pair + 1)

        last = len(SPANS) - 1
        round_y(last, on_scalar, 0, QUARTER // 2)
        quantize_y(last - 1)
        round_y(last, on_vector, QUARTER // 2, QUARTER)
        quantize_y(last)
        store_scales(GROUPS // 2, GROUPS, [nc.scalar, nc.scalar, nc.sync, nc.sync])
